import numpy as np
import ml_dtypes


def mxq(x, axis, fmt="e4m3"):
    dtype, down = {"e4m3": (ml_dtypes.float8_e4m3fn, 7), "e5m2": (ml_dtypes.float8_e5m2, 14)}[fmt]
    v = np.moveaxis(np.asarray(x, np.float32).astype(ml_dtypes.bfloat16).astype(np.float64), axis, -1)
    blocks = v.reshape(v.shape[:-1] + (-1, 32))
    amax = np.abs(blocks).max(-1, keepdims=True)
    byte = np.maximum(np.where(amax > 0, np.frexp(amax)[1] - 1 + 127, 0) - down, 1)
    scale = np.exp2(byte - 127.0)
    codes = (blocks / scale).astype(np.float32).astype(dtype).astype(np.float64)
    return np.moveaxis((codes * scale).reshape(v.shape), -1, axis)


WIDE = False


def mx_kscale(k):
    if not WIDE:
        return np.ones(k)
    levels = np.array([10, -10, 5, -5, 0])
    if k % 512:
        return np.exp2(np.random.permutation(np.resize(levels, k // 32))).repeat(32)
    a = np.empty((k // 512, 16))
    for p in range(k // 512):
        a[p, :8] = np.random.permutation(np.resize(levels, 8))
        for g in range(8):
            far = levels[np.abs(levels - a[p, g]) >= 10]
            a[p, g + 8] = far[np.random.randint(len(far))]
    return np.exp2(a.ravel()).repeat(32)


def f64(x):
    return np.asarray(x).astype(np.float64)


def striped(idx):
    return np.tile(np.asarray(idx).reshape(-1, 16).T, (8, 1)).astype(np.uint16)


def unstriped(offs):
    return offs[:16].T.reshape(-1).astype(np.int64)


E2M1 = np.array([0.0, 0.5, 1.0, 1.5, 2.0, 3.0, 4.0, 6.0, -0.0, -0.5, -1.0, -1.5, -2.0, -3.0, -4.0, -6.0])


def pack_weight(w, fmt):
    k, n = w.shape
    w = f64(np.asarray(w, np.float32).astype(ml_dtypes.bfloat16)).reshape(k // 32, 32, n)
    amax = np.abs(w).max(1)
    if fmt == "e4m3":
        byte = np.frexp(amax)[1] - 1 + 127 - 7
    else:
        mant, ex = np.frexp(amax / 6.0)
        byte = np.where(mant > 0.5, ex, ex - 1) + 127
    byte = np.clip(np.where(amax > 0, byte, 1), 1, 254)
    scaled = (w * np.exp2(127.0 - byte)[:, None, :]).reshape(k, n).astype(np.float32)
    by_word = np.ascontiguousarray(scaled.reshape(k // 512, 128, 4, n).transpose(0, 1, 3, 2))
    if fmt == "e4m3":
        words = by_word.astype(ml_dtypes.float8_e4m3fn).view(np.uint8)
    else:
        c = by_word.astype(ml_dtypes.float4_e2m1fn).view(np.uint8) & 0xF
        words = (c[..., 0::2] | (c[..., 1::2] << 4)).reshape(k // 512, 128, 2 * n)
    return np.ascontiguousarray(words), np.ascontiguousarray(byte.astype(np.uint8).reshape(k // 512, 16, n))


def unpack_weight(words, scales, fmt):
    g, _, n = scales.shape
    words = np.ascontiguousarray(words).reshape(g, 128, n, -1)
    if fmt == "e4m3":
        vals = words.view(ml_dtypes.float8_e4m3fn).astype(np.float64)
    else:
        nib = np.empty((g, 128, n, 4), np.uint8)
        nib[..., 0::2] = words & 0xF
        nib[..., 1::2] = words >> 4
        vals = E2M1[nib]
    vals = vals * np.repeat(np.exp2(scales.astype(np.float64) - 127.0), 8, axis=1)[..., None]
    return vals.transpose(0, 1, 3, 2).reshape(g * 512, n)


K, T, J, N = 1024, 2048, 512, 512


def setup_inputs():
    n = np.random.standard_normal
    idx = np.random.permutation(T)[:J]
    idx2 = np.random.permutation(T)[:J]
    fk = mx_kscale(K)
    xtp = pack_weight(n((K, T)) * np.random.uniform(0.3, 1.7, (1, T)) / fk[:, None], "e4m3")
    wbp = pack_weight(n((K, N)) * 1 / np.sqrt(K) * fk[:, None], "e2m1")
    return {
        "xt_words": xtp[0],
        "xt_scales": xtp[1],
        "wa": (n((K, N)) * 1 / np.sqrt(K) * fk[:, None]).astype(np.float32),
        "wb_words": wbp[0],
        "wb_scales": wbp[1],
        "of": (np.random.uniform(0.0, 1.5, (1, N))).astype(np.float32),
        "offs": striped(idx),
        "offs2": striped(idx2),
    }


def reference(xt_words, xt_scales, wa, wb_words, wb_scales, of, offs, offs2):
    idx = unstriped(offs)
    idx2 = unstriped(offs2)
    xtu = unpack_weight(xt_words, xt_scales, "e4m3")
    wbu = unpack_weight(wb_words, wb_scales, "e2m1")
    xtidxg = xtu[:, idx]
    waq = mxq(f64(wa), 0, "e4m3")
    a = xtidxg.T @ waq
    xtidx2g = xtu[:, idx2]
    b = xtidx2g.T @ wbu
    m = np.max(b, axis=1, keepdims=True)
    y = np.maximum(a + f64(of) - m + 3.0, 0.0)
    return y

@@ -1,0 +1,156 @@
+from contextlib import ExitStack
+
+import concourse.mybir as mybir
+from concourse.masks import make_identity
+
+K, T, J, N = 1024, 2048, 512, 512
+FLOPS = 2 * 2 * K * J * N
+
+F32 = mybir.dt.float32
+BF16 = mybir.dt.bfloat16
+I32 = mybir.dt.int32
+U32 = mybir.dt.uint32
+U16 = mybir.dt.uint16
+U8 = mybir.dt.uint8
+FP8X4 = mybir.dt.float8_e4m3fn_x4
+FP4X4 = mybir.dt.float4_e2m1fn_x4
+ALU = mybir.AluOpType
+ACT = mybir.ActivationFunctionType
+
+P = 128
+PACK = 4
+PASSES = 2
+TILES = J // P
+HALF = N // 2
+
+
+def tile_moe_expert_rows_against_best_of_other_kernel(
+    tc, xt_words, xt_scales, wa, wb_words, wb_scales, of, offs, offs2, out
+):
+    nc = tc.nc
+    with ExitStack() as ctx:
+        keep = ctx.enter_context(tc.tile_pool(name="keep", bufs=1))
+        psum = ctx.enter_context(tc.psum_pool(name="psum", bufs=1))
+
+        list_a = keep.tile([P, J // 16], U16, name="list_a")
+        list_b = keep.tile([P, J // 16], U16, name="list_b")
+        x_scales = keep.tile([P, T], U8, name="x_scales", align_bytes=64)
+        wb_plane = keep.tile([P, PASSES, N], U8, name="wb_plane", align_bytes=64)
+        b_scales1 = keep.tile([P, J], U8, name="b_scales1", align_bytes=64)
+        nc.gpsimd.memset(x_scales[:].bitcast(I32), 0)
+        nc.vector.memset(wb_plane[:].bitcast(I32), 0)
+        nc.vector.memset(b_scales1[:].bitcast(I32), 0)
+
+        nc.sync.dma_start(list_b[:], offs2)
+        of_cols = keep.tile([P, PACK], F32, name="of_cols")
+        nc.scalar.dma_start(of_cols[:], of.rearrange("o (p c) -> (o p) c", c=PACK))
+        for q in range(4):
+            nc.sync.dma_start(
+                x_scales[32 * q : 32 * q + 8, :].bitcast(I32),
+                xt_scales[:, 4 * q : 4 * q + 4, :].bitcast(I32),
+            )
+        nc.sync.dma_start(list_a[:], offs)
+        x_words = []
+        for z in range(PASSES):
+            w = keep.tile([P, T], I32, name="x_words%d" % z, align_bytes=64)
+            nc.sync.dma_start(w[:], xt_words[z].rearrange("p c r -> p (c r)").bitcast(I32))
+            x_words.append(w)
+
+        wb_codes = keep.tile([P, PASSES, 2 * N], U8, name="wb_codes", align_bytes=64)
+        nc.sync.dma_start(wb_codes[:].bitcast(I32), wb_words.rearrange("z p c -> p z c").bitcast(I32))
+        for r in range(4):
+            nc.sync.dma_start(
+                wb_plane[r:P:32, :, :].bitcast(I32),
+                wb_scales[:, r:16:4, :].rearrange("z q c -> q z c").bitcast(I32),
+            )
+        wa_raw = {}
+        for z in range(PASSES):
+            for h in range(2):
+                raw = keep.tile([P, PACK, HALF], F32, name="wa_raw%d%d" % (z, h))
+                rows = wa[z * 512 : (z + 1) * 512, h * HALF : (h + 1) * HALF]
+                nc.sync.dma_start(raw[:], rows.rearrange("(p t) n -> p t n", t=PACK))
+                wa_raw[(z, h)] = raw
+
+        ident = keep.tile([P, P], F32, name="ident")
+        make_identity(nc, ident[:])
+        of_ps = psum.tile([P, PACK, P], F32, name="of_ps", tag="a3")
+        for c in range(PACK):
+            nc.tensor.transpose(of_ps[:, c, :], of_cols[:, c : c + 1].to_broadcast([P, P]), ident[:])
+        of3 = keep.tile([P, N], F32, name="of3")
+        nc.scalar.activation(
+            of3[:].rearrange("q (p c) -> q p c", c=PACK), of_ps[:].rearrange("q c p -> q p c"), ACT.Copy, bias=3.0
+        )
+
+        b_scales = keep.tile([P, J], U8, name="b_scales", align_bytes=64)
+        a_scales = keep.tile([P, J], U8, name="a_scales", align_bytes=64)
+        nc.vector.tensor_copy(b_scales[:], x_scales[:].indirect(list_b[:]))
+        nc.scalar.dma_start(b_scales1[0:112, :].bitcast(I32), b_scales[4:116, :].bitcast(I32))
+        nc.vector.tensor_copy(a_scales[:], x_scales[:].indirect(list_a[:]))
+        a_words, b_words = [], []
+        for z in range(PASSES):
+            gb = keep.tile([P, J], U32, name="b_words%d" % z, align_bytes=64)
+            nc.vector.tensor_copy(gb[:], x_words[z][:].bitcast(U32).indirect(list_b[:]))
+            ga = keep.tile([P, J], U32, name="a_words%d" % z, align_bytes=64)
+            nc.vector.tensor_copy(ga[:], x_words[z][:].bitcast(U32).indirect(list_a[:]))
+            a_words.append(ga)
+            b_words.append(gb)
+
+        b_ps = [psum.tile([P, N], F32, name="b%d" % j) for j in range(TILES)]
+        b_planes = [b_scales, b_scales1]
+        for z in range(PASSES):
+            for j in range(TILES):
+                cols = slice(j * P, (j + 1) * P)
+                nc.tensor.matmul_mx(
+                    out=b_ps[j][:],
+                    lhsT=b_words[z][:, cols].bitcast(FP8X4),
+                    lhsT_scale=b_planes[z][:, cols],
+                    rhs=wb_codes[:, z, :].bitcast(FP4X4),
+                    rhs_scale=wb_plane[:, z, :],
+                    start=(z == 0),
+                    stop=(z == PASSES - 1),
+                )
+        neg_max = [None] * TILES
+
+        def row_max(j, tag):
+            neg_max[j] = keep.tile([P, 1], F32, name="neg_max%d" % j, tag=tag, align_bytes=64)
+            nc.vector.tensor_reduce(neg_max[j][:], b_ps[j][:], axis=mybir.AxisListType.X, op=ALU.max, negate=True)
+
+        for j in range(TILES - 1):
+            row_max(j, "neg_max%d" % j)
+
+        a_ps = [psum.tile([P, N], F32, name="a_ps%d" % j, tag="a%d" % j) for j in range(TILES)]
+        for z in range(PASSES):
+            codes = keep.tile([P, N], U32, name="wa_codes%d" % z, align_bytes=64)
+            plane = keep.tile([P, N], U8, name="wa_plane%d" % z, align_bytes=64)
+            for h in range(2):
+                grouped = keep.tile([P, HALF, PACK], BF16, name="wa_bf%d%d" % (z, h), tag="wa_bf%d%d" % (z, h), align_bytes=64)
+                dst = grouped[:].rearrange("p (c i) t -> p c t i", i=4)
+                src = wa_raw[(z, h)][:].rearrange("p t (c i) -> p c t i", i=4)
+                if z == 1 and h == 1:
+                    nc.scalar.copy(dst[:, 0:32], src[:, 0:32])
+                    nc.vector.tensor_copy(dst[:, 32:64], src[:, 32:64])
+                else:
+                    nc.scalar.copy(dst, src)
+                ncols = slice(h * HALF, (h + 1) * HALF)
+                nc.vector.quantize_mx(
+                    out=codes[:, ncols].bitcast(FP8X4), scales=plane[:, ncols], in_=grouped[:].rearrange("p n t -> p (n t)")
+                )
+            for j in range(TILES):
+                cols = slice(j * P, (j + 1) * P)
+                nc.tensor.matmul_mx(
+                    out=a_ps[j][:],
+                    lhsT=a_words[z][:, cols].bitcast(FP8X4),
+                    lhsT_scale=a_scales[4 * z : P, cols],
+                    rhs=codes[:].bitcast(FP8X4),
+                    rhs_scale=plane[:],
+                    start=(z == 0),
+                    stop=(z == PASSES - 1),
+                )
+        row_max(TILES - 1, "wa_bf11")
+
+        for j in range(TILES):
+            summed = keep.tile([P, N], F32, name="summed%d" % j)
+            nc.vector.tensor_tensor(summed[:], a_ps[j][:], of3[:], ALU.add)
+            res = keep.tile([P, N], F32, name="res%d" % j)
+            nc.scalar.activation(res[:], summed[:], ACT.Relu, bias=neg_max[j][:])
+            nc.sync.dma_start(out[j * P : (j + 1) * P, :], res[:])

@@ -50,6 +50,13 @@ def tile_moe_expert_rows_against_best_of_other_kernel(
                 xt_scales[:, 4 * q : 4 * q + 4, :].bitcast(I32),
             )
         nc.sync.dma_start(list_a[:], offs)
+
+        def load_wb_scales(r):
+            nc.sync.dma_start(
+                wb_plane[r:P:32, :, :].bitcast(I32),
+                wb_scales[:, r:16:4, :].rearrange("z q c -> q z c").bitcast(I32),
+            )
+
         x_words = []
         for z in range(PASSES):
             w = keep.tile([P, T], I32, name="x_words%d" % z, align_bytes=64)
@@ -59,10 +66,7 @@ def tile_moe_expert_rows_against_best_of_other_kernel(
         wb_codes = keep.tile([P, PASSES, 2 * N], U8, name="wb_codes", align_bytes=64)
         nc.sync.dma_start(wb_codes[:].bitcast(I32), wb_words.rearrange("z p c -> p z c").bitcast(I32))
         for r in range(4):
-            nc.sync.dma_start(
-                wb_plane[r:P:32, :, :].bitcast(I32),
-                wb_scales[:, r:16:4, :].rearrange("z q c -> q z c").bitcast(I32),
-            )
+            load_wb_scales(r)
         wa_raw = {}
         for z in range(PASSES):
             for h in range(2):
@@ -74,12 +78,12 @@ def tile_moe_expert_rows_against_best_of_other_kernel(
         ident = keep.tile([P, P], F32, name="ident")
         make_identity(nc, ident[:])
         of_ps = psum.tile([P, PACK, P], F32, name="of_ps", tag="a3")
+        of3_cols = keep.tile([P, PACK], F32, name="of3_cols")
+        nc.scalar.activation(of3_cols[:], of_cols[:], ACT.Copy, bias=3.0)
         for c in range(PACK):
-            nc.tensor.transpose(of_ps[:, c, :], of_cols[:, c : c + 1].to_broadcast([P, P]), ident[:])
+            nc.tensor.transpose(of_ps[:, c, :], of3_cols[:, c : c + 1].to_broadcast([P, P]), ident[:])
         of3 = keep.tile([P, N], F32, name="of3")
-        nc.scalar.activation(
-            of3[:].rearrange("q (p c) -> q p c", c=PACK), of_ps[:].rearrange("q c p -> q p c"), ACT.Copy, bias=3.0
-        )
+        nc.scalar.copy(of3[:].rearrange("q (p c) -> q p c", c=PACK), of_ps[:].rearrange("q c p -> q p c"))
 
         b_scales = keep.tile([P, J], U8, name="b_scales", align_bytes=64)
         a_scales = keep.tile([P, J], U8, name="a_scales", align_bytes=64)
@@ -95,10 +99,10 @@ def tile_moe_expert_rows_against_best_of_other_kernel(
             a_words.append(ga)
             b_words.append(gb)
 
-        b_ps = [psum.tile([P, N], F32, name="b%d" % j) for j in range(TILES)]
+        b_ps = [psum.tile([P, N], F32, name="b%d" % j, tag="b%d" % j) for j in range(TILES)]
         b_planes = [b_scales, b_scales1]
-        for z in range(PASSES):
-            for j in range(TILES):
+        for j in range(TILES):
+            for z in range(PASSES):
                 cols = slice(j * P, (j + 1) * P)
                 nc.tensor.matmul_mx(
                     out=b_ps[j][:],
@@ -115,42 +119,70 @@ def tile_moe_expert_rows_against_best_of_other_kernel(
             neg_max[j] = keep.tile([P, 1], F32, name="neg_max%d" % j, tag=tag, align_bytes=64)
             nc.vector.tensor_reduce(neg_max[j][:], b_ps[j][:], axis=mybir.AxisListType.X, op=ALU.max, negate=True)
 
-        for j in range(TILES - 1):
-            row_max(j, "neg_max%d" % j)
+        wa_codes, wa_planes, a_ps = {}, {}, {}
 
-        a_ps = [psum.tile([P, N], F32, name="a_ps%d" % j, tag="a%d" % j) for j in range(TILES)]
-        for z in range(PASSES):
-            codes = keep.tile([P, N], U32, name="wa_codes%d" % z, align_bytes=64)
-            plane = keep.tile([P, N], U8, name="wa_plane%d" % z, align_bytes=64)
-            for h in range(2):
-                grouped = keep.tile([P, HALF, PACK], BF16, name="wa_bf%d%d" % (z, h), tag="wa_bf%d%d" % (z, h), align_bytes=64)
-                dst = grouped[:].rearrange("p (c i) t -> p c t i", i=4)
-                src = wa_raw[(z, h)][:].rearrange("p t (c i) -> p c t i", i=4)
-                if z == 1 and h == 1:
-                    nc.scalar.copy(dst[:, 0:32], src[:, 0:32])
-                    nc.vector.tensor_copy(dst[:, 32:64], src[:, 32:64])
-                else:
-                    nc.scalar.copy(dst, src)
-                ncols = slice(h * HALF, (h + 1) * HALF)
-                nc.vector.quantize_mx(
-                    out=codes[:, ncols].bitcast(FP8X4), scales=plane[:, ncols], in_=grouped[:].rearrange("p n t -> p (n t)")
-                )
-            for j in range(TILES):
-                cols = slice(j * P, (j + 1) * P)
-                nc.tensor.matmul_mx(
-                    out=a_ps[j][:],
-                    lhsT=a_words[z][:, cols].bitcast(FP8X4),
-                    lhsT_scale=a_scales[4 * z : P, cols],
-                    rhs=codes[:].bitcast(FP8X4),
-                    rhs_scale=plane[:],
-                    start=(z == 0),
-                    stop=(z == PASSES - 1),
-                )
-        row_max(TILES - 1, "wa_bf11")
+        def quantise(z, h):
+            grouped = keep.tile([P, HALF, PACK], BF16, name="wa_bf%d%d" % (z, h), tag="wa_bf%d%d" % (z, h), align_bytes=64)
+            nc.scalar.copy(
+                grouped[:].rearrange("p (c i) t -> p c t i", i=4),
+                wa_raw[(z, h)][:].rearrange("p t (c i) -> p c t i", i=4),
+            )
+            wa_codes[(z, h)] = keep.tile([P, HALF], U32, name="wa_codes%d%d" % (z, h), align_bytes=64)
+            wa_planes[(z, h)] = keep.tile([P, HALF], U8, name="wa_plane%d%d" % (z, h), align_bytes=64)
+            nc.vector.quantize_mx(
+                out=wa_codes[(z, h)][:].bitcast(FP8X4),
+                scales=wa_planes[(z, h)][:],
+                in_=grouped[:].rearrange("p n t -> p (n t)"),
+            )
 
+        def a_pass(z, h, j):
+            if z == 0:
+                a_ps[(h, j)] = psum.tile([P, HALF], F32, name="a_ps%d%d" % (h, j), tag="%s%d" % ("ab"[h], j))
+            cols = slice(j * P, (j + 1) * P)
+            nc.tensor.matmul_mx(
+                out=a_ps[(h, j)][:],
+                lhsT=a_words[z][:, cols].bitcast(FP8X4),
+                lhsT_scale=a_scales[4 * z : P, cols],
+                rhs=wa_codes[(z, h)][:].bitcast(FP8X4),
+                rhs_scale=wa_planes[(z, h)][:],
+                start=(z == 0),
+                stop=(z == PASSES - 1),
+            )
+
+        row_max(0, "neg_max0")
+        quantise(0, 0)
         for j in range(TILES):
-            summed = keep.tile([P, N], F32, name="summed%d" % j)
-            nc.vector.tensor_tensor(summed[:], a_ps[j][:], of3[:], ALU.add)
-            res = keep.tile([P, N], F32, name="res%d" % j)
-            nc.scalar.activation(res[:], summed[:], ACT.Relu, bias=neg_max[j][:])
-            nc.sync.dma_start(out[j * P : (j + 1) * P, :], res[:])
+            a_pass(0, 0, j)
+        row_max(1, "wa_bf00")
+        quantise(0, 1)
+        a_pass(0, 1, 0)
+        a_pass(0, 1, 1)
+        row_max(2, "wa_bf01")
+        a_pass(0, 1, 2)
+        quantise(1, 0)
+        for j in range(TILES):
+            a_pass(1, 0, j)
+        row_max(3, "wa_bf10")
+        a_pass(0, 1, 3)
+        quantise(1, 1)
+        for j in range(TILES):
+            a_pass(1, 1, j)
+
+        for h in range(2):
+            ncols = slice(h * HALF, (h + 1) * HALF)
+            for pair in range(2):
+                res = keep.tile([P, 2, HALF], F32, name="res%d%d" % (h, pair))
+                rows = out[2 * pair * P : (2 * pair + 2) * P, ncols].rearrange("(u p) n -> p u n", p=P)
+                last = h == 1 and pair == 1
+                for u in range(2):
+                    j = 2 * pair + u
+                    summed = keep.tile([P, HALF], F32, name="summed%d%d" % (h, j))
+                    nc.vector.tensor_tensor(summed[:], a_ps[(h, j)][:], of3[:, ncols], ALU.add)
+                    if last and u == 1:
+                        nc.vector.tensor_scalar(res[:, u, :], summed[:], neg_max[j][:], 0.0, ALU.add, ALU.max)
+                    else:
+                        nc.scalar.activation(res[:, u, :], summed[:], ACT.Relu, bias=neg_max[j][:])
+                    if last:
+                        nc.sync.dma_start(rows[:, u, :], res[:, u, :])
+                if not last:
+                    nc.sync.dma_start(rows, res[:])

@@ -35,28 +35,32 @@ def tile_moe_expert_rows_against_best_of_other_kernel(
         list_a = keep.tile([P, J // 16], U16, name="list_a")
         list_b = keep.tile([P, J // 16], U16, name="list_b")
         x_scales = keep.tile([P, T], U8, name="x_scales", align_bytes=64)
-        wb_plane = keep.tile([P, PASSES, N], U8, name="wb_plane", align_bytes=64)
         b_scales1 = keep.tile([P, J], U8, name="b_scales1", align_bytes=64)
         nc.gpsimd.memset(x_scales[:].bitcast(I32), 0)
-        nc.vector.memset(wb_plane[:].bitcast(I32), 0)
         nc.vector.memset(b_scales1[:].bitcast(I32), 0)
 
         nc.sync.dma_start(list_b[:], offs2)
-        of_cols = keep.tile([P, PACK], F32, name="of_cols")
+        of_cols = keep.tile([P, PACK], F32, name="of_cols", tag="wb_plane", align_bytes=64)
         nc.scalar.dma_start(of_cols[:], of.rearrange("o (p c) -> (o p) c", c=PACK))
         for q in range(4):
-            nc.sync.dma_start(
+            (nc.scalar if q == 3 else nc.sync).dma_start(
                 x_scales[32 * q : 32 * q + 8, :].bitcast(I32),
                 xt_scales[:, 4 * q : 4 * q + 4, :].bitcast(I32),
             )
         nc.sync.dma_start(list_a[:], offs)
+        of3_cols = keep.tile([P, PACK], F32, name="of3_cols")
+        nc.scalar.activation(of3_cols[:], of_cols[:], ACT.Copy, bias=3.0)
+        wb_plane = keep.tile([P, PASSES, N], U8, name="wb_plane", tag="wb_plane", align_bytes=64)
+        nc.vector.memset(wb_plane[:].bitcast(I32), 0)
 
-        def load_wb_scales(r):
-            nc.sync.dma_start(
+        def load_wb_scales(queue, r):
+            queue.dma_start(
                 wb_plane[r:P:32, :, :].bitcast(I32),
                 wb_scales[:, r:16:4, :].rearrange("z q c -> q z c").bitcast(I32),
             )
 
+        for r in range(2):
+            load_wb_scales(nc.scalar, r)
         x_words = []
         for z in range(PASSES):
             w = keep.tile([P, T], I32, name="x_words%d" % z, align_bytes=64)
@@ -65,12 +69,12 @@ def tile_moe_expert_rows_against_best_of_other_kernel(
 
         wb_codes = keep.tile([P, PASSES, 2 * N], U8, name="wb_codes", align_bytes=64)
         nc.sync.dma_start(wb_codes[:].bitcast(I32), wb_words.rearrange("z p c -> p z c").bitcast(I32))
-        for r in range(4):
-            load_wb_scales(r)
+        for r in range(2, 4):
+            load_wb_scales(nc.sync, r)
         wa_raw = {}
         for z in range(PASSES):
             for h in range(2):
-                raw = keep.tile([P, PACK, HALF], F32, name="wa_raw%d%d" % (z, h))
+                raw = keep.tile([P, PACK, HALF], F32, name="wa_raw%d%d" % (z, h), tag="wa_raw%d%d" % (z, h))
                 rows = wa[z * 512 : (z + 1) * 512, h * HALF : (h + 1) * HALF]
                 nc.sync.dma_start(raw[:], rows.rearrange("(p t) n -> p t n", t=PACK))
                 wa_raw[(z, h)] = raw
@@ -78,8 +82,6 @@ def tile_moe_expert_rows_against_best_of_other_kernel(
         ident = keep.tile([P, P], F32, name="ident")
         make_identity(nc, ident[:])
         of_ps = psum.tile([P, PACK, P], F32, name="of_ps", tag="a3")
-        of3_cols = keep.tile([P, PACK], F32, name="of3_cols")
-        nc.scalar.activation(of3_cols[:], of_cols[:], ACT.Copy, bias=3.0)
         for c in range(PACK):
             nc.tensor.transpose(of_ps[:, c, :], of3_cols[:, c : c + 1].to_broadcast([P, P]), ident[:])
         of3 = keep.tile([P, N], F32, name="of3")
@@ -171,17 +173,19 @@ def tile_moe_expert_rows_against_best_of_other_kernel(
         for h in range(2):
             ncols = slice(h * HALF, (h + 1) * HALF)
             for pair in range(2):
-                res = keep.tile([P, 2, HALF], F32, name="res%d%d" % (h, pair))
+                res_tag = "wa_raw11" if (h, pair) == (0, 0) else "res%d%d" % (h, pair)
+                res = keep.tile([P, 2, HALF], F32, name="res%d%d" % (h, pair), tag=res_tag)
+                sum_tag = "wa_bf11" if (h, pair) == (0, 1) else "summed%d%d" % (h, pair)
+                summed = keep.tile([P, 2, HALF], F32, name="summed%d%d" % (h, pair), tag=sum_tag, align_bytes=64)
                 rows = out[2 * pair * P : (2 * pair + 2) * P, ncols].rearrange("(u p) n -> p u n", p=P)
                 last = h == 1 and pair == 1
                 for u in range(2):
                     j = 2 * pair + u
-                    summed = keep.tile([P, HALF], F32, name="summed%d%d" % (h, j))
-                    nc.vector.tensor_tensor(summed[:], a_ps[(h, j)][:], of3[:, ncols], ALU.add)
+                    nc.vector.tensor_tensor(summed[:, u, :], a_ps[(h, j)][:], of3[:, ncols], ALU.add)
                     if last and u == 1:
-                        nc.vector.tensor_scalar(res[:, u, :], summed[:], neg_max[j][:], 0.0, ALU.add, ALU.max)
+                        nc.vector.tensor_scalar(res[:, u, :], summed[:, u, :], neg_max[j][:], 0.0, ALU.add, ALU.max)
                     else:
-                        nc.scalar.activation(res[:, u, :], summed[:], ACT.Relu, bias=neg_max[j][:])
+                        nc.scalar.activation(res[:, u, :], summed[:, u, :], ACT.Relu, bias=neg_max[j][:])
                     if last:
                         nc.sync.dma_start(rows[:, u, :], res[:, u, :])
                 if not last:

from contextlib import ExitStack

import concourse.mybir as mybir
from concourse.masks import make_identity

K, T, J, N = 1024, 2048, 512, 512
FLOPS = 2 * 2 * K * J * N

F32 = mybir.dt.float32
BF16 = mybir.dt.bfloat16
I32 = mybir.dt.int32
U32 = mybir.dt.uint32
U16 = mybir.dt.uint16
U8 = mybir.dt.uint8
FP8X4 = mybir.dt.float8_e4m3fn_x4
FP4X4 = mybir.dt.float4_e2m1fn_x4
ALU = mybir.AluOpType
ACT = mybir.ActivationFunctionType

P = 128
PACK = 4
PASSES = 2
TILES = J // P
HALF = N // 2


def tile_moe_expert_rows_against_best_of_other_kernel(
    tc, xt_words, xt_scales, wa, wb_words, wb_scales, of, offs, offs2, out
):
    nc = tc.nc
    with ExitStack() as ctx:
        keep = ctx.enter_context(tc.tile_pool(name="keep", bufs=1))
        psum = ctx.enter_context(tc.psum_pool(name="psum", bufs=1))

        list_a = keep.tile([P, J // 16], U16, name="list_a")
        list_b = keep.tile([P, J // 16], U16, name="list_b")
        x_scales = keep.tile([P, T], U8, name="x_scales", align_bytes=64)
        b_scales1 = keep.tile([P, J], U8, name="b_scales1", align_bytes=64)
        nc.gpsimd.memset(x_scales[:].bitcast(I32), 0)
        nc.vector.memset(b_scales1[:].bitcast(I32), 0)

        nc.sync.dma_start(list_b[:], offs2)
        of_cols = keep.tile([P, PACK], F32, name="of_cols", tag="wb_plane", align_bytes=64)
        nc.scalar.dma_start(of_cols[:], of.rearrange("o (p c) -> (o p) c", c=PACK))
        for q in range(4):
            (nc.scalar if q == 3 else nc.sync).dma_start(
                x_scales[32 * q : 32 * q + 8, :].bitcast(I32),
                xt_scales[:, 4 * q : 4 * q + 4, :].bitcast(I32),
            )
        nc.sync.dma_start(list_a[:], offs)
        of3_cols = keep.tile([P, PACK], F32, name="of3_cols")
        nc.scalar.activation(of3_cols[:], of_cols[:], ACT.Copy, bias=3.0)
        wb_plane = keep.tile([P, PASSES, N], U8, name="wb_plane", tag="wb_plane", align_bytes=64)
        nc.vector.memset(wb_plane[:].bitcast(I32), 0)

        def load_wb_scales(queue, r):
            queue.dma_start(
                wb_plane[r:P:32, :, :].bitcast(I32),
                wb_scales[:, r:16:4, :].rearrange("z q c -> q z c").bitcast(I32),
            )

        for r in range(2):
            load_wb_scales(nc.scalar, r)
        x_words = []
        for z in range(PASSES):
            w = keep.tile([P, T], I32, name="x_words%d" % z, align_bytes=64)
            nc.sync.dma_start(w[:], xt_words[z].rearrange("p c r -> p (c r)").bitcast(I32))
            x_words.append(w)

        wb_codes = keep.tile([P, PASSES, 2 * N], U8, name="wb_codes", align_bytes=64)
        nc.sync.dma_start(wb_codes[:].bitcast(I32), wb_words.rearrange("z p c -> p z c").bitcast(I32))
        for r in range(2, 4):
            load_wb_scales(nc.sync, r)
        wa_raw = {}
        for z in range(PASSES):
            for h in range(2):
                raw = keep.tile([P, PACK, HALF], F32, name="wa_raw%d%d" % (z, h), tag="wa_raw%d%d" % (z, h))
                rows = wa[z * 512 : (z + 1) * 512, h * HALF : (h + 1) * HALF]
                nc.sync.dma_start(raw[:], rows.rearrange("(p t) n -> p t n", t=PACK))
                wa_raw[(z, h)] = raw

        ident = keep.tile([P, P], F32, name="ident")
        make_identity(nc, ident[:])
        of_ps = psum.tile([P, PACK, P], F32, name="of_ps", tag="a3")
        for c in range(PACK):
            nc.tensor.transpose(of_ps[:, c, :], of3_cols[:, c : c + 1].to_broadcast([P, P]), ident[:])
        of3 = keep.tile([P, N], F32, name="of3")
        nc.scalar.copy(of3[:].rearrange("q (p c) -> q p c", c=PACK), of_ps[:].rearrange("q c p -> q p c"))

        b_scales = keep.tile([P, J], U8, name="b_scales", align_bytes=64)
        a_scales = keep.tile([P, J], U8, name="a_scales", align_bytes=64)
        nc.vector.tensor_copy(b_scales[:], x_scales[:].indirect(list_b[:]))
        nc.scalar.dma_start(b_scales1[0:112, :].bitcast(I32), b_scales[4:116, :].bitcast(I32))
        nc.vector.tensor_copy(a_scales[:], x_scales[:].indirect(list_a[:]))
        a_words, b_words = [], []
        for z in range(PASSES):
            gb = keep.tile([P, J], U32, name="b_words%d" % z, align_bytes=64)
            nc.vector.tensor_copy(gb[:], x_words[z][:].bitcast(U32).indirect(list_b[:]))
            ga = keep.tile([P, J], U32, name="a_words%d" % z, align_bytes=64)
            nc.vector.tensor_copy(ga[:], x_words[z][:].bitcast(U32).indirect(list_a[:]))
            a_words.append(ga)
            b_words.append(gb)

        b_ps = [psum.tile([P, N], F32, name="b%d" % j, tag="b%d" % j) for j in range(TILES)]
        b_planes = [b_scales, b_scales1]
        for j in range(TILES):
            for z in range(PASSES):
                cols = slice(j * P, (j + 1) * P)
                nc.tensor.matmul_mx(
                    out=b_ps[j][:],
                    lhsT=b_words[z][:, cols].bitcast(FP8X4),
                    lhsT_scale=b_planes[z][:, cols],
                    rhs=wb_codes[:, z, :].bitcast(FP4X4),
                    rhs_scale=wb_plane[:, z, :],
                    start=(z == 0),
                    stop=(z == PASSES - 1),
                )
        neg_max = [None] * TILES

        def row_max(j, tag):
            neg_max[j] = keep.tile([P, 1], F32, name="neg_max%d" % j, tag=tag, align_bytes=64)
            nc.vector.tensor_reduce(neg_max[j][:], b_ps[j][:], axis=mybir.AxisListType.X, op=ALU.max, negate=True)

        wa_codes, wa_planes, a_ps = {}, {}, {}

        def quantise(z, h):
            grouped = keep.tile([P, HALF, PACK], BF16, name="wa_bf%d%d" % (z, h), tag="wa_bf%d%d" % (z, h), align_bytes=64)
            nc.scalar.copy(
                grouped[:].rearrange("p (c i) t -> p c t i", i=4),
                wa_raw[(z, h)][:].rearrange("p t (c i) -> p c t i", i=4),
            )
            wa_codes[(z, h)] = keep.tile([P, HALF], U32, name="wa_codes%d%d" % (z, h), align_bytes=64)
            wa_planes[(z, h)] = keep.tile([P, HALF], U8, name="wa_plane%d%d" % (z, h), align_bytes=64)
            nc.vector.quantize_mx(
                out=wa_codes[(z, h)][:].bitcast(FP8X4),
                scales=wa_planes[(z, h)][:],
                in_=grouped[:].rearrange("p n t -> p (n t)"),
            )

        def a_pass(z, h, j):
            if z == 0:
                a_ps[(h, j)] = psum.tile([P, HALF], F32, name="a_ps%d%d" % (h, j), tag="%s%d" % ("ab"[h], j))
            cols = slice(j * P, (j + 1) * P)
            nc.tensor.matmul_mx(
                out=a_ps[(h, j)][:],
                lhsT=a_words[z][:, cols].bitcast(FP8X4),
                lhsT_scale=a_scales[4 * z : P, cols],
                rhs=wa_codes[(z, h)][:].bitcast(FP8X4),
                rhs_scale=wa_planes[(z, h)][:],
                start=(z == 0),
                stop=(z == PASSES - 1),
            )

        row_max(0, "neg_max0")
        quantise(0, 0)
        for j in range(TILES):
            a_pass(0, 0, j)
        row_max(1, "wa_bf00")
        quantise(0, 1)
        a_pass(0, 1, 0)
        a_pass(0, 1, 1)
        row_max(2, "wa_bf01")
        a_pass(0, 1, 2)
        quantise(1, 0)
        for j in range(TILES):
            a_pass(1, 0, j)
        row_max(3, "wa_bf10")
        a_pass(0, 1, 3)
        quantise(1, 1)
        for j in range(TILES):
            a_pass(1, 1, j)

        for h in range(2):
            ncols = slice(h * HALF, (h + 1) * HALF)
            for pair in range(2):
                res_tag = "wa_raw11" if (h, pair) == (0, 0) else "res%d%d" % (h, pair)
                res = keep.tile([P, 2, HALF], F32, name="res%d%d" % (h, pair), tag=res_tag)
                sum_tag = "wa_bf11" if (h, pair) == (0, 1) else "summed%d%d" % (h, pair)
                summed = keep.tile([P, 2, HALF], F32, name="summed%d%d" % (h, pair), tag=sum_tag, align_bytes=64)
                rows = out[2 * pair * P : (2 * pair + 2) * P, ncols].rearrange("(u p) n -> p u n", p=P)
                last = h == 1 and pair == 1
                for u in range(2):
                    j = 2 * pair + u
                    nc.vector.tensor_tensor(summed[:, u, :], a_ps[(h, j)][:], of3[:, ncols], ALU.add)
                    if last and u == 1:
                        nc.vector.tensor_scalar(res[:, u, :], summed[:, u, :], neg_max[j][:], 0.0, ALU.add, ALU.max)
                    else:
                        nc.scalar.activation(res[:, u, :], summed[:, u, :], ACT.Relu, bias=neg_max[j][:])
                    if last:
                        nc.sync.dma_start(rows[:, u, :], res[:, u, :])
                if not last:
                    nc.sync.dma_start(rows, res[:])
